import numpy as np
import ml_dtypes


def mxq(x, axis, fmt="e4m3"):
    dtype, down = {"e4m3": (ml_dtypes.float8_e4m3fn, 7), "e5m2": (ml_dtypes.float8_e5m2, 14)}[fmt]
    v = np.moveaxis(np.asarray(x, np.float32).astype(ml_dtypes.bfloat16).astype(np.float64), axis, -1)
    blocks = v.reshape(v.shape[:-1] + (-1, 32))
    amax = np.abs(blocks).max(-1, keepdims=True)
    byte = np.maximum(np.where(amax > 0, np.frexp(amax)[1] - 1 + 127, 0) - down, 1)
    scale = np.exp2(byte - 127.0)
    codes = (blocks / scale).astype(np.float32).astype(dtype).astype(np.float64)
    return np.moveaxis((codes * scale).reshape(v.shape), -1, axis)


WIDE = False


def mx_kscale(k):
    if not WIDE:
        return np.ones(k)
    levels = np.array([10, -10, 5, -5, 0])
    if k % 512:
        return np.exp2(np.random.permutation(np.resize(levels, k // 32))).repeat(32)
    a = np.empty((k // 512, 16))
    for p in range(k // 512):
        a[p, :8] = np.random.permutation(np.resize(levels, 8))
        for g in range(8):
            far = levels[np.abs(levels - a[p, g]) >= 10]
            a[p, g + 8] = far[np.random.randint(len(far))]
    return np.exp2(a.ravel()).repeat(32)


def f64(x):
    return np.asarray(x).astype(np.float64)


def striped(idx):
    return np.tile(np.asarray(idx).reshape(-1, 16).T, (8, 1)).astype(np.uint16)


def unstriped(offs):
    return offs[:16].T.reshape(-1).astype(np.int64)


E2M1 = np.array([0.0, 0.5, 1.0, 1.5, 2.0, 3.0, 4.0, 6.0, -0.0, -0.5, -1.0, -1.5, -2.0, -3.0, -4.0, -6.0])


def pack_weight(w, fmt):
    k, n = w.shape
    w = f64(np.asarray(w, np.float32).astype(ml_dtypes.bfloat16)).reshape(k // 32, 32, n)
    amax = np.abs(w).max(1)
    if fmt == "e4m3":
        byte = np.frexp(amax)[1] - 1 + 127 - 7
    else:
        mant, ex = np.frexp(amax / 6.0)
        byte = np.where(mant > 0.5, ex, ex - 1) + 127
    byte = np.clip(np.where(amax > 0, byte, 1), 1, 254)
    scaled = (w * np.exp2(127.0 - byte)[:, None, :]).reshape(k, n).astype(np.float32)
    by_word = np.ascontiguousarray(scaled.reshape(k // 512, 128, 4, n).transpose(0, 1, 3, 2))
    if fmt == "e4m3":
        words = by_word.astype(ml_dtypes.float8_e4m3fn).view(np.uint8)
    else:
        c = by_word.astype(ml_dtypes.float4_e2m1fn).view(np.uint8) & 0xF
        words = (c[..., 0::2] | (c[..., 1::2] << 4)).reshape(k // 512, 128, 2 * n)
    return np.ascontiguousarray(words), np.ascontiguousarray(byte.astype(np.uint8).reshape(k // 512, 16, n))


def unpack_weight(words, scales, fmt):
    g, _, n = scales.shape
    words = np.ascontiguousarray(words).reshape(g, 128, n, -1)
    if fmt == "e4m3":
        vals = words.view(ml_dtypes.float8_e4m3fn).astype(np.float64)
    else:
        nib = np.empty((g, 128, n, 4), np.uint8)
        nib[..., 0::2] = words & 0xF
        nib[..., 1::2] = words >> 4
        vals = E2M1[nib]
    vals = vals * np.repeat(np.exp2(scales.astype(np.float64) - 127.0), 8, axis=1)[..., None]
    return vals.transpose(0, 1, 3, 2).reshape(g * 512, n)


D, T, I, J, U, Z, E = 512, 2048, 512, 512, 1024, 1024, 512


def setup_inputs():
    n = np.random.standard_normal
    idx = np.random.permutation(T)[:I]
    idx2 = np.random.permutation(U)[:J]
    idx3 = np.random.permutation(Z)[:J]
    fd = mx_kscale(D)
    fi = mx_kscale(I)
    ti = np.ones(T)
    ti[idx] = fi
    keysp = pack_weight(n((D, T)) / fd[:, None], "e4m3")
    return {
        "keys_words": keysp[0],
        "keys_scales": keysp[1],
        "notes": (n((D, U)) * 1.0 / np.sqrt(D) * fd[:, None]).astype(np.float32),
        "users2": (n((D, Z)) * 1.0 / np.sqrt(D) * fd[:, None]).astype(np.float32),
        "rowf": (np.random.uniform(0.02, 0.08, (I, 1)) * fi[:, None]).astype(np.float32),
        "vals": (n((E, T)) / ti).astype(np.float32),
        "mem": (np.random.uniform(0.3, 1.0, (1, J))).astype(np.float32),
        "offs": striped(idx),
        "offs2": striped(idx2),
        "offs3": striped(idx3),
    }


def reference(keys_words, keys_scales, notes, users2, rowf, vals, mem, offs, offs2, offs3):
    idx = unstriped(offs)
    idx2 = unstriped(offs2)
    idx3 = unstriped(offs3)
    keysu = unpack_weight(keys_words, keys_scales, "e4m3")
    keysidxg = keysu[:, idx]
    notesidx2q = mxq(f64(notes)[:, idx2], 0, "e4m3")
    g1 = keysidxg.T @ notesidx2q
    users2idx3q = mxq(f64(users2)[:, idx3], 0, "e4m3")
    g2 = keysidxg.T @ users2idx3q
    g0 = np.maximum(g1, g2)
    gr1 = g0 * f64(rowf)
    vt1 = f64(vals)[:, idx].T
    vt1q = mxq(vt1, 0, "e4m3")
    gr1q = mxq(gr1, 0, "e4m3")
    o = vt1q.T @ gr1q
    o1 = np.pad(o, ((0, 0), (1, 0)))[:, :J]
    y = o - o1 * f64(mem)
    return y

@@ -1,0 +1,274 @@
+from contextlib import ExitStack
+
+import concourse.mybir as mybir
+from concourse.masks import make_identity
+
+D, T, I, J, U, E = 512, 2048, 512, 512, 1024, 512
+FLOPS = 2 * 2 * D * I * J + 2 * I * E * J
+BYTES = D * T + (D // 32) * T + 2 * D * U * 4 + E * T * 4 + (I + J) * 4 + 3 * 128 * 32 * 2 + E * J * 4
+
+F32 = mybir.dt.float32
+BF16 = mybir.dt.bfloat16
+I32 = mybir.dt.int32
+U32 = mybir.dt.uint32
+U16 = mybir.dt.uint16
+U8 = mybir.dt.uint8
+FP8X4 = mybir.dt.float8_e4m3fn_x4
+COPY = mybir.ActivationFunctionType.Copy
+ALU = mybir.AluOpType
+
+P = 128
+PACK = 4
+CHUNK = 128
+CHUNKS = J // CHUNK
+BLOCKS = E // P
+
+
+def tile_attend_tab_larger_changes_kernel(
+    tc, keys_words, keys_scales, notes, users2, rowf, vals, mem, offs, offs2, offs3, out
+):
+    nc = tc.nc
+    with ExitStack() as ctx:
+        keep = ctx.enter_context(tc.tile_pool(name="keep", bufs=1))
+        psum = ctx.enter_context(tc.psum_pool(name="psum", bufs=1))
+
+        def sb(shape, dtype, name, tag=""):
+            return keep.tile(shape, dtype, name=name, tag=tag or name, align_bytes=64)
+
+        def bank(shape, index):
+            return psum.tile(shape, F32, name="bank%d" % index, tag="bank%d" % index)
+
+        token_list = sb([P, I // 16], U16, "token_list")
+        note_list = sb([P, J // 16], U16, "note_list")
+        user_list = sb([P, J // 16], U16, "user_list")
+        key_pool = sb([P, T], I32, "key_pool")
+        key_scale_pool = sb([P, T], U8, "key_scale_pool")
+        note_pool = [sb([P, U], F32, "note_pool%d" % t) for t in range(PACK)]
+        user_pool = [sb([P, U], F32, "user_pool%d" % t) for t in range(PACK)]
+        val_pool = [sb([P, T], F32, "val_pool%d" % b) for b in range(BLOCKS)]
+        row_factor = sb([P, 1, PACK], F32, "row_factor")
+        mem_cols = sb([P, PACK], F32, "mem_cols")
+        ident = sb([P, P], F32, "ident")
+
+        nc.gpsimd.memset(key_scale_pool[:].bitcast(I32), 0)
+        make_identity(nc, ident[:])
+
+        note_planes = notes.rearrange("(p t) u -> t p u", t=PACK)
+        user_planes = users2.rearrange("(p t) u -> t p u", t=PACK)
+        nc.sync.dma_start(note_list[:], offs2)
+        nc.sync.dma_start(note_pool[0][:], note_planes[0])
+        nc.sync.dma_start(token_list[:], offs)
+        for q in range(4):
+            nc.sync.dma_start(
+                key_scale_pool[32 * q : 32 * q + 4, :].bitcast(I32),
+                keys_scales[0, 4 * q : 4 * q + 4, :].bitcast(I32),
+            )
+        for t in range(1, PACK):
+            nc.sync.dma_start(note_pool[t][:], note_planes[t])
+        nc.sync.dma_start(mem_cols[:], mem.rearrange("o (p c) -> p (o c)", c=PACK))
+        nc.sync.dma_start(key_pool[:], keys_words[0].rearrange("p n t -> p (n t)").bitcast(I32))
+        nc.sync.dma_start(user_list[:], offs3)
+        nc.sync.dma_start(row_factor[:], rowf.rearrange("(p t) o -> p o t", t=PACK))
+        for t in range(PACK):
+            nc.sync.dma_start(user_pool[t][:], user_planes[t])
+        for b in range(BLOCKS):
+            nc.sync.dma_start(val_pool[b][:], vals[b * P : (b + 1) * P, :])
+
+        def gather(on_scalar, dst, pool, offsets):
+            if on_scalar:
+                nc.scalar.activation(dst, pool[:].indirect(offsets), COPY)
+            else:
+                nc.vector.tensor_copy(dst, pool[:].indirect(offsets))
+
+        def interleave(on_scalar, grouped, planes):
+            copy = nc.scalar.copy if on_scalar else nc.vector.tensor_copy
+            copy(grouped.rearrange("p (c i) t -> p c t i", i=4), planes.rearrange("p t (c i) -> p c t i", i=4))
+
+        halves = [slice(0, J // 2), slice(J // 2, J)]
+        list_halves = [slice(0, J // 32), slice(J // 32, J // 16)]
+
+        def quantize(codes, scales, grouped):
+            nc.vector.quantize_mx(out=codes.bitcast(FP8X4), scales=scales, in_=grouped)
+
+        def gather_planes(cols, pools, offsets, planes):
+            for t in planes:
+                for h in range(2):
+                    gather(h == 1, cols[h][:, t, :], pools[t], offsets[:, list_halves[h]])
+
+        def quantize_half(h, codes, scales, grouped):
+            quantize(codes[h][:], scales[h][:], grouped[h][:].rearrange("p j t -> p (j t)"))
+
+        note_cols = [sb([P, PACK, J // 2], BF16, "note_cols%d" % h, "B" if h == 0 else "") for h in range(2)]
+        gather_planes(note_cols, note_pool, note_list, range(1))
+        key_scales = sb([P, I], U8, "key_scales")
+        nc.vector.tensor_copy(
+            key_scales[:].rearrange("p (r s) -> p s r", r=PACK), key_scale_pool[:].indirect(token_list[:])
+        )
+        gather_planes(note_cols, note_pool, note_list, range(1, PACK))
+        note_grouped = [sb([P, J // 2, PACK], BF16, "note_grouped%d" % h) for h in range(2)]
+        for h in range(2):
+            interleave(h == 1, note_grouped[h][:], note_cols[h][:])
+
+        mem_bank = bank([P, PACK, P], 0)
+        for c in range(PACK):
+            nc.tensor.transpose(mem_bank[:, c, :], mem_cols[:, c : c + 1].to_broadcast([P, P]), ident[:])
+        mem_rows = sb([P, J], F32, "mem_rows")
+        nc.scalar.copy(mem_rows[:].rearrange("m (p c) -> m p c", c=PACK), mem_bank[:].rearrange("m c p -> m p c"))
+        shifted = sb([P, BLOCKS, J], F32, "shifted")
+        nc.vector.memset(shifted[:, :, 0:1], 0.0)
+
+        note_codes = [sb([P, J // 2], U32, "note_codes%d" % h) for h in range(2)]
+        note_scales = [sb([P, J // 2], U8, "note_scales%d" % h) for h in range(2)]
+        quantize_half(0, note_codes, note_scales, note_grouped)
+
+        key_codes = sb([P, I], U32, "key_codes", "B")
+        nc.vector.tensor_copy(
+            key_codes[:].rearrange("p (r s) -> p s r", r=PACK),
+            key_pool[:].bitcast(U32).indirect(token_list[:]),
+        )
+        quantize_half(1, note_codes, note_scales, note_grouped)
+
+        def scores(codes, scales, c, index):
+            acc = bank([P, PACK, CHUNK], index)
+            h = c // 2
+            cols = slice(c % 2 * CHUNK, (c % 2 + 1) * CHUNK)
+            for r in range(PACK):
+                rows = slice(r * P, (r + 1) * P)
+                nc.tensor.matmul_mx(
+                    out=acc[:, r, :],
+                    lhsT=key_codes[:, rows].bitcast(FP8X4),
+                    lhsT_scale=key_scales[:, rows],
+                    rhs=codes[h][:, cols].bitcast(FP8X4),
+                    rhs_scale=scales[h][:, cols],
+                    start=True,
+                    stop=True,
+                )
+            return acc
+
+        g1 = [sb([P, CHUNK, PACK], F32, "g1_%d" % c, "F" if c == 1 else "") for c in range(CHUNKS)]
+        g0 = [sb([P, CHUNK, PACK], F32, "g0_%d" % c) for c in range(CHUNKS)]
+
+        user_cols = [sb([P, PACK, J // 2], BF16, "user_cols%d" % h, "D" if h == 1 else "") for h in range(2)]
+        for t in range(2):
+            for h in range(2):
+                gather(t == 0, user_cols[h][:, t, :], user_pool[t], user_list[:, list_halves[h]])
+        for c in range(CHUNKS):
+            acc = scores(note_codes, note_scales, c, c)
+            nc.scalar.copy(g1[c][:], acc[:].rearrange("s r j -> s j r"))
+        gather_planes(user_cols, user_pool, user_list, range(2, PACK))
+        user_grouped = [sb([P, J // 2, PACK], BF16, "user_grouped%d" % h, "C" if h == 1 else "") for h in range(2)]
+        user_codes = [sb([P, J // 2], U32, "user_codes0")]
+        user_scales = [sb([P, J // 2], U8, "user_scales%d" % h) for h in range(2)]
+        for h in range(2):
+            interleave(h == 1, user_grouped[h][:], user_cols[h][:])
+
+        table_grouped = sb([P, J, PACK], BF16, "table_grouped")
+        table_codes = sb([P, J], U32, "table_codes")
+        table_scales = sb([P, J], U8, "table_scales")
+
+        def larger(c):
+            acc = scores(user_codes, user_scales, c, CHUNKS + c)
+            nc.vector.tensor_tensor(g0[c][:], acc[:].rearrange("s r j -> s j r"), g1[c][:], ALU.max)
+
+        def weigh(c):
+            nc.vector.tensor_tensor(
+                table_grouped[:, c * CHUNK : (c + 1) * CHUNK, :],
+                g0[c][:],
+                row_factor[:].to_broadcast([P, CHUNK, PACK]),
+                ALU.mult,
+            )
+
+        def quantize_table(h):
+            quantize(
+                table_codes[:, halves[h]],
+                table_scales[:, halves[h]],
+                table_grouped[:, halves[h], :].rearrange("p j t -> p (j t)"),
+            )
+
+        groups = [(0, 2), (2, 3), (3, 4)]
+        val_codes = sb([P, E], U32, "val_codes")
+        val_scales = sb([P, E], U8, "val_scales")
+        val_grouped = [sb([P, b1 - b0, P, 2], F32, "val_grouped%d" % b0, "E" if b0 == 0 else "") for b0, b1 in groups]
+
+        def turn_values(g, index):
+            b0, b1 = groups[g]
+            cols = []
+            for b in range(b0, b1):
+                val_cols = sb([P, I], BF16, "val_cols%d" % b, ["D", "C", "D", "E"][b])
+                gather(True, val_cols[:], val_pool[b], token_list[:])
+                cols.append(val_cols)
+            turned = bank([P, b1 - b0, 2, P], index)
+            for b in range(b0, b1):
+                words = cols[b - b0][:].bitcast(F32)
+                for u in range(2):
+                    nc.tensor.transpose(turned[:, b - b0, u, :], words[:, u : I // 2 : 2], ident[:])
+            nc.scalar.copy(val_grouped[g][:], turned[:].rearrange("p b u e -> p b e u"))
+
+        def quantize_values(g):
+            b0, b1 = groups[g]
+            cols = slice(b0 * P, b1 * P)
+            quantize(
+                val_codes[:, cols],
+                val_scales[:, cols],
+                val_grouped[g][:].rearrange("p b e u -> p (b e u)").bitcast(BF16),
+            )
+
+        quantize_half(0, user_codes, user_scales, user_grouped)
+        larger(0)
+        larger(1)
+        user_codes.append(sb([P, J // 2], U32, "user_codes1", "F"))
+        weigh(0)
+        quantize_half(1, user_codes, user_scales, user_grouped)
+        weigh(1)
+        quantize_table(0)
+        larger(2)
+        larger(3)
+        turn_values(0, CHUNKS + 2)
+        weigh(2)
+        weigh(3)
+        quantize_table(1)
+        quantize_values(0)
+        turn_values(1, 1)
+
+        sums = []
+
+        def multiply(b):
+            acc = bank([P, J], b)
+            nc.tensor.matmul_mx(
+                out=acc[:],
+                lhsT=val_codes[:, b * P : (b + 1) * P].bitcast(FP8X4),
+                lhsT_scale=val_scales[:, b * P : (b + 1) * P],
+                rhs=table_codes[:].bitcast(FP8X4),
+                rhs_scale=table_scales[:],
+                start=True,
+                stop=True,
+            )
+            sums.append(acc)
+
+        def shift(b, j0, j1):
+            j0 = max(j0, 1)
+            nc.vector.tensor_tensor(shifted[:, b, j0:j1], sums[b][:, j0 - 1 : j1 - 1], mem_rows[:, j0:j1], ALU.mult)
+
+        results = [sb([P, J], F32, "result%d" % b) for b in range(BLOCKS)]
+
+        def finish(b, j0, j1):
+            nc.vector.tensor_tensor(results[b][:, j0:j1], sums[b][:, j0:j1], shifted[:, b, j0:j1], ALU.subtract)
+            nc.sync.dma_start(out[b * P : (b + 1) * P, j0:j1], results[b][:, j0:j1])
+
+        multiply(0)
+        multiply(1)
+        shift(0, 0, J)
+        quantize_values(1)
+        finish(0, 0, J)
+        shift(1, 0, J)
+        turn_values(2, CHUNKS)
+        multiply(2)
+        finish(1, 0, J)
+        shift(2, 0, J)
+        quantize_values(2)
+        multiply(3)
+        finish(2, 0, J)
+        shift(3, 0, J // 2)
+        shift(3, J // 2, J)
+        finish(3, 0, J // 2)
+        finish(3, J // 2, J)

@@ -30,6 +30,7 @@ def tile_attend_tab_larger_changes_kernel(
     nc = tc.nc
     with ExitStack() as ctx:
         keep = ctx.enter_context(tc.tile_pool(name="keep", bufs=1))
+        late = ctx.enter_context(tc.tile_pool(name="late", bufs=1))
         psum = ctx.enter_context(tc.psum_pool(name="psum", bufs=1))
 
         def sb(shape, dtype, name, tag=""):
@@ -41,7 +42,7 @@ def tile_attend_tab_larger_changes_kernel(
         token_list = sb([P, I // 16], U16, "token_list")
         note_list = sb([P, J // 16], U16, "note_list")
         user_list = sb([P, J // 16], U16, "user_list")
-        key_pool = sb([P, T], I32, "key_pool")
+        key_pool = sb([P, T], I32, "key_pool", "A")
         key_scale_pool = sb([P, T], U8, "key_scale_pool")
         note_pool = [sb([P, U], F32, "note_pool%d" % t) for t in range(PACK)]
         user_pool = [sb([P, U], F32, "user_pool%d" % t) for t in range(PACK)]
@@ -84,7 +85,6 @@ def tile_attend_tab_larger_changes_kernel(
             copy = nc.scalar.copy if on_scalar else nc.vector.tensor_copy
             copy(grouped.rearrange("p (c i) t -> p c t i", i=4), planes.rearrange("p t (c i) -> p c t i", i=4))
 
-        halves = [slice(0, J // 2), slice(J // 2, J)]
         list_halves = [slice(0, J // 32), slice(J // 32, J // 16)]
 
         def quantize(codes, scales, grouped):
@@ -98,35 +98,36 @@ def tile_attend_tab_larger_changes_kernel(
         def quantize_half(h, codes, scales, grouped):
             quantize(codes[h][:], scales[h][:], grouped[h][:].rearrange("p j t -> p (j t)"))
 
-        note_cols = [sb([P, PACK, J // 2], BF16, "note_cols%d" % h, "B" if h == 0 else "") for h in range(2)]
+        note_cols = [sb([P, PACK, J // 2], BF16, "note_cols%d" % h) for h in range(2)]
         gather_planes(note_cols, note_pool, note_list, range(1))
         key_scales = sb([P, I], U8, "key_scales")
         nc.vector.tensor_copy(
             key_scales[:].rearrange("p (r s) -> p s r", r=PACK), key_scale_pool[:].indirect(token_list[:])
         )
         gather_planes(note_cols, note_pool, note_list, range(1, PACK))
-        note_grouped = [sb([P, J // 2, PACK], BF16, "note_grouped%d" % h) for h in range(2)]
+        note_grouped = [sb([P, J // 2, PACK], BF16, "note_grouped%d" % h, "B" if h == 1 else "") for h in range(2)]
         for h in range(2):
             interleave(h == 1, note_grouped[h][:], note_cols[h][:])
 
         mem_bank = bank([P, PACK, P], 0)
         for c in range(PACK):
             nc.tensor.transpose(mem_bank[:, c, :], mem_cols[:, c : c + 1].to_broadcast([P, P]), ident[:])
-        mem_rows = sb([P, J], F32, "mem_rows")
+        mem_rows = sb([P, J], F32, "mem_rows", "note_cols1")
         nc.scalar.copy(mem_rows[:].rearrange("m (p c) -> m p c", c=PACK), mem_bank[:].rearrange("m c p -> m p c"))
-        shifted = sb([P, BLOCKS, J], F32, "shifted")
-        nc.vector.memset(shifted[:, :, 0:1], 0.0)
+        shifted = [sb([P, J], F32, "shifted%d" % b) for b in range(BLOCKS)]
+        for b in range(BLOCKS):
+            nc.vector.memset(shifted[b][:, 0:1], 0.0)
 
         note_codes = [sb([P, J // 2], U32, "note_codes%d" % h) for h in range(2)]
         note_scales = [sb([P, J // 2], U8, "note_scales%d" % h) for h in range(2)]
-        quantize_half(0, note_codes, note_scales, note_grouped)
+        for h in range(2):
+            quantize_half(h, note_codes, note_scales, note_grouped)
 
         key_codes = sb([P, I], U32, "key_codes", "B")
         nc.vector.tensor_copy(
             key_codes[:].rearrange("p (r s) -> p s r", r=PACK),
             key_pool[:].bitcast(U32).indirect(token_list[:]),
         )
-        quantize_half(1, note_codes, note_scales, note_grouped)
 
         def scores(codes, scales, c, index):
             acc = bank([P, PACK, CHUNK], index)
@@ -145,24 +146,29 @@ def tile_attend_tab_larger_changes_kernel(
                 )
             return acc
 
-        g1 = [sb([P, CHUNK, PACK], F32, "g1_%d" % c, "F" if c == 1 else "") for c in range(CHUNKS)]
+        g1 = [sb([P, CHUNK, PACK], F32, "g1_%d" % c) for c in range(CHUNKS)]
         g0 = [sb([P, CHUNK, PACK], F32, "g0_%d" % c) for c in range(CHUNKS)]
 
-        user_cols = [sb([P, PACK, J // 2], BF16, "user_cols%d" % h, "D" if h == 1 else "") for h in range(2)]
+        user_both = sb([P, 2, PACK, J // 2], BF16, "user_both", "A")
+        user_cols = [user_both[:, h] for h in range(2)]
         for t in range(2):
             for h in range(2):
                 gather(t == 0, user_cols[h][:, t, :], user_pool[t], user_list[:, list_halves[h]])
-        for c in range(CHUNKS):
+
+        def note_scores(c):
             acc = scores(note_codes, note_scales, c, c)
             nc.scalar.copy(g1[c][:], acc[:].rearrange("s r j -> s j r"))
-        gather_planes(user_cols, user_pool, user_list, range(2, PACK))
-        user_grouped = [sb([P, J // 2, PACK], BF16, "user_grouped%d" % h, "C" if h == 1 else "") for h in range(2)]
-        user_codes = [sb([P, J // 2], U32, "user_codes0")]
-        user_scales = [sb([P, J // 2], U8, "user_scales%d" % h) for h in range(2)]
-        for h in range(2):
-            interleave(h == 1, user_grouped[h][:], user_cols[h][:])
 
-        table_grouped = sb([P, J, PACK], BF16, "table_grouped")
+        note_scores(0)
+        note_scores(1)
+        gather_planes(user_cols, user_pool, user_list, range(2, PACK))
+        user_grouped = []
+        user_codes = [sb([P, J // 2], U32, "user_codes%d" % h) for h in range(2)]
+        user_scales = [sb([P, J // 2], U8, "user_scales%d" % h) for h in range(2)]
+        note_scores(2)
+        note_scores(3)
+
+        table_grouped = late.tile([P, J, PACK], BF16, name="table_grouped", align_bytes=64, offset=0)
         table_codes = sb([P, J], U32, "table_codes")
         table_scales = sb([P, J], U8, "table_scales")
 
@@ -171,30 +177,27 @@ def tile_attend_tab_larger_changes_kernel(
             nc.vector.tensor_tensor(g0[c][:], acc[:].rearrange("s r j -> s j r"), g1[c][:], ALU.max)
 
         def weigh(c):
-            nc.vector.tensor_tensor(
+            engine = nc.gpsimd if c < 2 else nc.vector
+            engine.tensor_tensor(
                 table_grouped[:, c * CHUNK : (c + 1) * CHUNK, :],
                 g0[c][:],
                 row_factor[:].to_broadcast([P, CHUNK, PACK]),
                 ALU.mult,
             )
 
-        def quantize_table(h):
-            quantize(
-                table_codes[:, halves[h]],
-                table_scales[:, halves[h]],
-                table_grouped[:, halves[h], :].rearrange("p j t -> p (j t)"),
-            )
-
-        groups = [(0, 2), (2, 3), (3, 4)]
-        val_codes = sb([P, E], U32, "val_codes")
+        groups = [(0, 2), (2, 4)]
+        val_codes = {}
         val_scales = sb([P, E], U8, "val_scales")
-        val_grouped = [sb([P, b1 - b0, P, 2], F32, "val_grouped%d" % b0, "E" if b0 == 0 else "") for b0, b1 in groups]
+        val_grouped = [sb([P, b1 - b0, P, 2], F32, "val_grouped%d" % b0) for b0, b1 in groups]
 
         def turn_values(g, index):
             b0, b1 = groups[g]
             cols = []
             for b in range(b0, b1):
-                val_cols = sb([P, I], BF16, "val_cols%d" % b, ["D", "C", "D", "E"][b])
+                if b == BLOCKS - 1:
+                    val_cols = late.tile([P, I], BF16, name="val_cols_last", align_bytes=64, offset=0)
+                else:
+                    val_cols = sb([P, I], BF16, "val_cols%d" % b, "note_codes1" if b == 0 else "note_codes0")
                 gather(True, val_cols[:], val_pool[b], token_list[:])
                 cols.append(val_cols)
             turned = bank([P, b1 - b0, 2, P], index)
@@ -207,28 +210,30 @@ def tile_attend_tab_larger_changes_kernel(
         def quantize_values(g):
             b0, b1 = groups[g]
             cols = slice(b0 * P, b1 * P)
+            if g == 1:
+                codes = late.tile([P, 2 * P], U32, name="val_codes_third", align_bytes=64, offset=2 * I)
+            else:
+                codes = sb([P, 2 * P], U32, "val_codes")
+            for b in range(b0, b1):
+                val_codes[b] = codes[:, (b - b0) * P : (b - b0 + 1) * P]
             quantize(
-                val_codes[:, cols],
+                codes[:],
                 val_scales[:, cols],
                 val_grouped[g][:].rearrange("p b e u -> p (b e u)").bitcast(BF16),
             )
 
-        quantize_half(0, user_codes, user_scales, user_grouped)
-        larger(0)
-        larger(1)
-        user_codes.append(sb([P, J // 2], U32, "user_codes1", "F"))
-        weigh(0)
-        quantize_half(1, user_codes, user_scales, user_grouped)
-        weigh(1)
-        quantize_table(0)
-        larger(2)
-        larger(3)
-        turn_values(0, CHUNKS + 2)
-        weigh(2)
-        weigh(3)
-        quantize_table(1)
+        for h in range(2):
+            user_grouped.append(sb([P, J // 2, PACK], BF16, "user_grouped"))
+            interleave(False, user_grouped[h][:], user_cols[h])
+            quantize_half(h, user_codes, user_scales, user_grouped)
+        for c in range(CHUNKS):
+            larger(c)
+        for c in range(CHUNKS):
+            weigh(c)
+        turn_values(0, CHUNKS)
+        quantize(table_codes[:], table_scales[:], table_grouped[:].rearrange("p j t -> p (j t)"))
         quantize_values(0)
-        turn_values(1, 1)
+        turn_values(1, CHUNKS + 1)
 
         sums = []
 
@@ -236,7 +241,7 @@ def tile_attend_tab_larger_changes_kernel(
             acc = bank([P, J], b)
             nc.tensor.matmul_mx(
                 out=acc[:],
-                lhsT=val_codes[:, b * P : (b + 1) * P].bitcast(FP8X4),
+                lhsT=val_codes[b].bitcast(FP8X4),
                 lhsT_scale=val_scales[:, b * P : (b + 1) * P],
                 rhs=table_codes[:].bitcast(FP8X4),
                 rhs_scale=table_scales[:],
@@ -247,28 +252,24 @@ def tile_attend_tab_larger_changes_kernel(
 
         def shift(b, j0, j1):
             j0 = max(j0, 1)
-            nc.vector.tensor_tensor(shifted[:, b, j0:j1], sums[b][:, j0 - 1 : j1 - 1], mem_rows[:, j0:j1], ALU.mult)
+            nc.vector.tensor_tensor(shifted[b][:, j0:j1], sums[b][:, j0 - 1 : j1 - 1], mem_rows[:, j0:j1], ALU.mult)
 
         results = [sb([P, J], F32, "result%d" % b) for b in range(BLOCKS)]
 
         def finish(b, j0, j1):
-            nc.vector.tensor_tensor(results[b][:, j0:j1], sums[b][:, j0:j1], shifted[:, b, j0:j1], ALU.subtract)
+            nc.vector.tensor_tensor(results[b][:, j0:j1], sums[b][:, j0:j1], shifted[b][:, j0:j1], ALU.subtract)
             nc.sync.dma_start(out[b * P : (b + 1) * P, j0:j1], results[b][:, j0:j1])
 
         multiply(0)
         multiply(1)
         shift(0, 0, J)
-        quantize_values(1)
-        finish(0, 0, J)
         shift(1, 0, J)
-        turn_values(2, CHUNKS)
+        finish(0, 0, J)
+        quantize_values(1)
         multiply(2)
+        multiply(3)
         finish(1, 0, J)
         shift(2, 0, J)
-        quantize_values(2)
-        multiply(3)
+        shift(3, 0, J)
         finish(2, 0, J)
-        shift(3, 0, J // 2)
-        shift(3, J // 2, J)
-        finish(3, 0, J // 2)
-        finish(3, J // 2, J)
+        finish(3, 0, J)

@@ -30,7 +30,10 @@ def tile_attend_tab_larger_changes_kernel(
     nc = tc.nc
     with ExitStack() as ctx:
         keep = ctx.enter_context(tc.tile_pool(name="keep", bufs=1))
+        early = ctx.enter_context(tc.tile_pool(name="early", bufs=1))
+        middle = ctx.enter_context(tc.tile_pool(name="middle", bufs=1))
         late = ctx.enter_context(tc.tile_pool(name="late", bufs=1))
+        last = ctx.enter_context(tc.tile_pool(name="last", bufs=1))
         psum = ctx.enter_context(tc.psum_pool(name="psum", bufs=1))
 
         def sb(shape, dtype, name, tag=""):
@@ -42,10 +45,11 @@ def tile_attend_tab_larger_changes_kernel(
         token_list = sb([P, I // 16], U16, "token_list")
         note_list = sb([P, J // 16], U16, "note_list")
         user_list = sb([P, J // 16], U16, "user_list")
-        key_pool = sb([P, T], I32, "key_pool", "A")
+        key_pool = early.tile([P, T], I32, name="key_pool", align_bytes=64, offset=0)
         key_scale_pool = sb([P, T], U8, "key_scale_pool")
         note_pool = [sb([P, U], F32, "note_pool%d" % t) for t in range(PACK)]
-        user_pool = [sb([P, U], F32, "user_pool%d" % t) for t in range(PACK)]
+        user_pool = [sb([P, U], F32, "user_pool%d" % t) for t in range(PACK - 1)]
+        user_pool.append(middle.tile([P, U], F32, name="user_pool_last", align_bytes=64, offset=1024))
         val_pool = [sb([P, T], F32, "val_pool%d" % b) for b in range(BLOCKS)]
         row_factor = sb([P, 1, PACK], F32, "row_factor")
         mem_cols = sb([P, PACK], F32, "mem_cols")
@@ -146,14 +150,23 @@ def tile_attend_tab_larger_changes_kernel(
                 )
             return acc
 
-        g1 = [sb([P, CHUNK, PACK], F32, "g1_%d" % c) for c in range(CHUNKS)]
+        g1 = [sb([P, CHUNK, PACK], F32, "g1_0")]
+        for c in range(1, CHUNKS):
+            g1.append(middle.tile([P, CHUNK, PACK], F32, name="g1_%d" % c, align_bytes=64, offset=(c - 1) * 2048))
         g0 = [sb([P, CHUNK, PACK], F32, "g0_%d" % c) for c in range(CHUNKS)]
 
-        user_both = sb([P, 2, PACK, J // 2], BF16, "user_both", "A")
-        user_cols = [user_both[:, h] for h in range(2)]
-        for t in range(2):
-            for h in range(2):
-                gather(t == 0, user_cols[h][:, t, :], user_pool[t], user_list[:, list_halves[h]])
+        user_grouped = [
+            early.tile([P, J // 2, PACK], BF16, name="user_grouped0", align_bytes=64, offset=0),
+            sb([P, J // 2, PACK], BF16, "user_grouped1"),
+        ]
+        user_cols = early.tile([P, PACK, J // 2], BF16, name="user_cols", align_bytes=64, offset=4 * J)
+
+        def gather_users(t):
+            gather(False, user_grouped[0][:, :, t], user_pool[t], user_list[:, list_halves[0]])
+            gather(True, user_cols[:, t, :], user_pool[t], user_list[:, list_halves[1]])
+
+        gather_users(0)
+        gather_users(1)
 
         def note_scores(c):
             acc = scores(note_codes, note_scales, c, c)
@@ -161,8 +174,8 @@ def tile_attend_tab_larger_changes_kernel(
 
         note_scores(0)
         note_scores(1)
-        gather_planes(user_cols, user_pool, user_list, range(2, PACK))
-        user_grouped = []
+        gather_users(2)
+        gather_users(3)
         user_codes = [sb([P, J // 2], U32, "user_codes%d" % h) for h in range(2)]
         user_scales = [sb([P, J // 2], U8, "user_scales%d" % h) for h in range(2)]
         note_scores(2)
@@ -188,16 +201,19 @@ def tile_attend_tab_larger_changes_kernel(
         groups = [(0, 2), (2, 4)]
         val_codes = {}
         val_scales = sb([P, E], U8, "val_scales")
-        val_grouped = [sb([P, b1 - b0, P, 2], F32, "val_grouped%d" % b0) for b0, b1 in groups]
+        val_grouped = [last.tile([P, 2, P, 2], F32, name="val_grouped0", align_bytes=64, offset=0)]
+        val_grouped.append(sb([P, 2, P, 2], F32, "val_grouped1"))
 
         def turn_values(g, index):
             b0, b1 = groups[g]
             cols = []
             for b in range(b0, b1):
-                if b == BLOCKS - 1:
-                    val_cols = late.tile([P, I], BF16, name="val_cols_last", align_bytes=64, offset=0)
+                if b == 3:
+                    val_cols = last.tile([P, I], BF16, name="val_cols3", align_bytes=64, offset=0)
+                elif b >= 1:
+                    val_cols = sb([P, I], BF16, "val_cols%d" % b, "g1_0")
                 else:
-                    val_cols = sb([P, I], BF16, "val_cols%d" % b, "note_codes1" if b == 0 else "note_codes0")
+                    val_cols = early.tile([P, I], BF16, name="val_cols0", align_bytes=64, offset=4 * J)
                 gather(True, val_cols[:], val_pool[b], token_list[:])
                 cols.append(val_cols)
             turned = bank([P, b1 - b0, 2, P], index)
@@ -210,10 +226,10 @@ def tile_attend_tab_larger_changes_kernel(
         def quantize_values(g):
             b0, b1 = groups[g]
             cols = slice(b0 * P, b1 * P)
-            if g == 1:
-                codes = late.tile([P, 2 * P], U32, name="val_codes_third", align_bytes=64, offset=2 * I)
+            if g == 0:
+                codes = late.tile([P, 2 * P], U32, name="val_codes0", align_bytes=64, offset=0)
             else:
-                codes = sb([P, 2 * P], U32, "val_codes")
+                codes = sb([P, 2 * P], U32, "val_codes1")
             for b in range(b0, b1):
                 val_codes[b] = codes[:, (b - b0) * P : (b - b0 + 1) * P]
             quantize(
@@ -222,15 +238,14 @@ def tile_attend_tab_larger_changes_kernel(
                 val_grouped[g][:].rearrange("p b e u -> p (b e u)").bitcast(BF16),
             )
 
+        interleave(False, user_grouped[1][:], user_cols[:])
         for h in range(2):
-            user_grouped.append(sb([P, J // 2, PACK], BF16, "user_grouped"))
-            interleave(False, user_grouped[h][:], user_cols[h])
             quantize_half(h, user_codes, user_scales, user_grouped)
         for c in range(CHUNKS):
             larger(c)
         for c in range(CHUNKS):
             weigh(c)
-        turn_values(0, CHUNKS)
+        turn_values(0, CHUNKS + 2)
         quantize(table_codes[:], table_scales[:], table_grouped[:].rearrange("p j t -> p (j t)"))
         quantize_values(0)
         turn_values(1, CHUNKS + 1)

from contextlib import ExitStack

import concourse.mybir as mybir
from concourse.masks import make_identity

D, T, I, J, U, E = 512, 2048, 512, 512, 1024, 512
FLOPS = 2 * 2 * D * I * J + 2 * I * E * J
BYTES = D * T + (D // 32) * T + 2 * D * U * 4 + E * T * 4 + (I + J) * 4 + 3 * 128 * 32 * 2 + E * J * 4

F32 = mybir.dt.float32
BF16 = mybir.dt.bfloat16
I32 = mybir.dt.int32
U32 = mybir.dt.uint32
U16 = mybir.dt.uint16
U8 = mybir.dt.uint8
FP8X4 = mybir.dt.float8_e4m3fn_x4
COPY = mybir.ActivationFunctionType.Copy
ALU = mybir.AluOpType

P = 128
PACK = 4
CHUNK = 128
CHUNKS = J // CHUNK
BLOCKS = E // P


def tile_attend_tab_larger_changes_kernel(
    tc, keys_words, keys_scales, notes, users2, rowf, vals, mem, offs, offs2, offs3, out
):
    nc = tc.nc
    with ExitStack() as ctx:
        keep = ctx.enter_context(tc.tile_pool(name="keep", bufs=1))
        early = ctx.enter_context(tc.tile_pool(name="early", bufs=1))
        middle = ctx.enter_context(tc.tile_pool(name="middle", bufs=1))
        late = ctx.enter_context(tc.tile_pool(name="late", bufs=1))
        last = ctx.enter_context(tc.tile_pool(name="last", bufs=1))
        psum = ctx.enter_context(tc.psum_pool(name="psum", bufs=1))

        def sb(shape, dtype, name, tag=""):
            return keep.tile(shape, dtype, name=name, tag=tag or name, align_bytes=64)

        def bank(shape, index):
            return psum.tile(shape, F32, name="bank%d" % index, tag="bank%d" % index)

        token_list = sb([P, I // 16], U16, "token_list")
        note_list = sb([P, J // 16], U16, "note_list")
        user_list = sb([P, J // 16], U16, "user_list")
        key_pool = early.tile([P, T], I32, name="key_pool", align_bytes=64, offset=0)
        key_scale_pool = sb([P, T], U8, "key_scale_pool")
        note_pool = [sb([P, U], F32, "note_pool%d" % t) for t in range(PACK)]
        user_pool = [sb([P, U], F32, "user_pool%d" % t) for t in range(PACK - 1)]
        user_pool.append(middle.tile([P, U], F32, name="user_pool_last", align_bytes=64, offset=1024))
        val_pool = [sb([P, T], F32, "val_pool%d" % b) for b in range(BLOCKS)]
        row_factor = sb([P, 1, PACK], F32, "row_factor")
        mem_cols = sb([P, PACK], F32, "mem_cols")
        ident = sb([P, P], F32, "ident")

        nc.gpsimd.memset(key_scale_pool[:].bitcast(I32), 0)
        make_identity(nc, ident[:])

        note_planes = notes.rearrange("(p t) u -> t p u", t=PACK)
        user_planes = users2.rearrange("(p t) u -> t p u", t=PACK)
        nc.sync.dma_start(note_list[:], offs2)
        nc.sync.dma_start(note_pool[0][:], note_planes[0])
        nc.sync.dma_start(token_list[:], offs)
        for q in range(4):
            nc.sync.dma_start(
                key_scale_pool[32 * q : 32 * q + 4, :].bitcast(I32),
                keys_scales[0, 4 * q : 4 * q + 4, :].bitcast(I32),
            )
        for t in range(1, PACK):
            nc.sync.dma_start(note_pool[t][:], note_planes[t])
        nc.sync.dma_start(mem_cols[:], mem.rearrange("o (p c) -> p (o c)", c=PACK))
        nc.sync.dma_start(key_pool[:], keys_words[0].rearrange("p n t -> p (n t)").bitcast(I32))
        nc.sync.dma_start(user_list[:], offs3)
        nc.sync.dma_start(row_factor[:], rowf.rearrange("(p t) o -> p o t", t=PACK))
        for t in range(PACK):
            nc.sync.dma_start(user_pool[t][:], user_planes[t])
        for b in range(BLOCKS):
            nc.sync.dma_start(val_pool[b][:], vals[b * P : (b + 1) * P, :])

        def gather(on_scalar, dst, pool, offsets):
            if on_scalar:
                nc.scalar.activation(dst, pool[:].indirect(offsets), COPY)
            else:
                nc.vector.tensor_copy(dst, pool[:].indirect(offsets))

        def interleave(on_scalar, grouped, planes):
            copy = nc.scalar.copy if on_scalar else nc.vector.tensor_copy
            copy(grouped.rearrange("p (c i) t -> p c t i", i=4), planes.rearrange("p t (c i) -> p c t i", i=4))

        list_halves = [slice(0, J // 32), slice(J // 32, J // 16)]

        def quantize(codes, scales, grouped):
            nc.vector.quantize_mx(out=codes.bitcast(FP8X4), scales=scales, in_=grouped)

        def gather_planes(cols, pools, offsets, planes):
            for t in planes:
                for h in range(2):
                    gather(h == 1, cols[h][:, t, :], pools[t], offsets[:, list_halves[h]])

        def quantize_half(h, codes, scales, grouped):
            quantize(codes[h][:], scales[h][:], grouped[h][:].rearrange("p j t -> p (j t)"))

        note_cols = [sb([P, PACK, J // 2], BF16, "note_cols%d" % h) for h in range(2)]
        gather_planes(note_cols, note_pool, note_list, range(1))
        key_scales = sb([P, I], U8, "key_scales")
        nc.vector.tensor_copy(
            key_scales[:].rearrange("p (r s) -> p s r", r=PACK), key_scale_pool[:].indirect(token_list[:])
        )
        gather_planes(note_cols, note_pool, note_list, range(1, PACK))
        note_grouped = [sb([P, J // 2, PACK], BF16, "note_grouped%d" % h, "B" if h == 1 else "") for h in range(2)]
        for h in range(2):
            interleave(h == 1, note_grouped[h][:], note_cols[h][:])

        mem_bank = bank([P, PACK, P], 0)
        for c in range(PACK):
            nc.tensor.transpose(mem_bank[:, c, :], mem_cols[:, c : c + 1].to_broadcast([P, P]), ident[:])
        mem_rows = sb([P, J], F32, "mem_rows", "note_cols1")
        nc.scalar.copy(mem_rows[:].rearrange("m (p c) -> m p c", c=PACK), mem_bank[:].rearrange("m c p -> m p c"))
        shifted = [sb([P, J], F32, "shifted%d" % b) for b in range(BLOCKS)]
        for b in range(BLOCKS):
            nc.vector.memset(shifted[b][:, 0:1], 0.0)

        note_codes = [sb([P, J // 2], U32, "note_codes%d" % h) for h in range(2)]
        note_scales = [sb([P, J // 2], U8, "note_scales%d" % h) for h in range(2)]
        for h in range(2):
            quantize_half(h, note_codes, note_scales, note_grouped)

        key_codes = sb([P, I], U32, "key_codes", "B")
        nc.vector.tensor_copy(
            key_codes[:].rearrange("p (r s) -> p s r", r=PACK),
            key_pool[:].bitcast(U32).indirect(token_list[:]),
        )

        def scores(codes, scales, c, index):
            acc = bank([P, PACK, CHUNK], index)
            h = c // 2
            cols = slice(c % 2 * CHUNK, (c % 2 + 1) * CHUNK)
            for r in range(PACK):
                rows = slice(r * P, (r + 1) * P)
                nc.tensor.matmul_mx(
                    out=acc[:, r, :],
                    lhsT=key_codes[:, rows].bitcast(FP8X4),
                    lhsT_scale=key_scales[:, rows],
                    rhs=codes[h][:, cols].bitcast(FP8X4),
                    rhs_scale=scales[h][:, cols],
                    start=True,
                    stop=True,
                )
            return acc

        g1 = [sb([P, CHUNK, PACK], F32, "g1_0")]
        for c in range(1, CHUNKS):
            g1.append(middle.tile([P, CHUNK, PACK], F32, name="g1_%d" % c, align_bytes=64, offset=(c - 1) * 2048))
        g0 = [sb([P, CHUNK, PACK], F32, "g0_%d" % c) for c in range(CHUNKS)]

        user_grouped = [
            early.tile([P, J // 2, PACK], BF16, name="user_grouped0", align_bytes=64, offset=0),
            sb([P, J // 2, PACK], BF16, "user_grouped1"),
        ]
        user_cols = early.tile([P, PACK, J // 2], BF16, name="user_cols", align_bytes=64, offset=4 * J)

        def gather_users(t):
            gather(False, user_grouped[0][:, :, t], user_pool[t], user_list[:, list_halves[0]])
            gather(True, user_cols[:, t, :], user_pool[t], user_list[:, list_halves[1]])

        gather_users(0)
        gather_users(1)

        def note_scores(c):
            acc = scores(note_codes, note_scales, c, c)
            nc.scalar.copy(g1[c][:], acc[:].rearrange("s r j -> s j r"))

        note_scores(0)
        note_scores(1)
        gather_users(2)
        gather_users(3)
        user_codes = [sb([P, J // 2], U32, "user_codes%d" % h) for h in range(2)]
        user_scales = [sb([P, J // 2], U8, "user_scales%d" % h) for h in range(2)]
        note_scores(2)
        note_scores(3)

        table_grouped = late.tile([P, J, PACK], BF16, name="table_grouped", align_bytes=64, offset=0)
        table_codes = sb([P, J], U32, "table_codes")
        table_scales = sb([P, J], U8, "table_scales")

        def larger(c):
            acc = scores(user_codes, user_scales, c, CHUNKS + c)
            nc.vector.tensor_tensor(g0[c][:], acc[:].rearrange("s r j -> s j r"), g1[c][:], ALU.max)

        def weigh(c):
            engine = nc.gpsimd if c < 2 else nc.vector
            engine.tensor_tensor(
                table_grouped[:, c * CHUNK : (c + 1) * CHUNK, :],
                g0[c][:],
                row_factor[:].to_broadcast([P, CHUNK, PACK]),
                ALU.mult,
            )

        groups = [(0, 2), (2, 4)]
        val_codes = {}
        val_scales = sb([P, E], U8, "val_scales")
        val_grouped = [last.tile([P, 2, P, 2], F32, name="val_grouped0", align_bytes=64, offset=0)]
        val_grouped.append(sb([P, 2, P, 2], F32, "val_grouped1"))

        def turn_values(g, index):
            b0, b1 = groups[g]
            cols = []
            for b in range(b0, b1):
                if b == 3:
                    val_cols = last.tile([P, I], BF16, name="val_cols3", align_bytes=64, offset=0)
                elif b >= 1:
                    val_cols = sb([P, I], BF16, "val_cols%d" % b, "g1_0")
                else:
                    val_cols = early.tile([P, I], BF16, name="val_cols0", align_bytes=64, offset=4 * J)
                gather(True, val_cols[:], val_pool[b], token_list[:])
                cols.append(val_cols)
            turned = bank([P, b1 - b0, 2, P], index)
            for b in range(b0, b1):
                words = cols[b - b0][:].bitcast(F32)
                for u in range(2):
                    nc.tensor.transpose(turned[:, b - b0, u, :], words[:, u : I // 2 : 2], ident[:])
            nc.scalar.copy(val_grouped[g][:], turned[:].rearrange("p b u e -> p b e u"))

        def quantize_values(g):
            b0, b1 = groups[g]
            cols = slice(b0 * P, b1 * P)
            if g == 0:
                codes = late.tile([P, 2 * P], U32, name="val_codes0", align_bytes=64, offset=0)
            else:
                codes = sb([P, 2 * P], U32, "val_codes1")
            for b in range(b0, b1):
                val_codes[b] = codes[:, (b - b0) * P : (b - b0 + 1) * P]
            quantize(
                codes[:],
                val_scales[:, cols],
                val_grouped[g][:].rearrange("p b e u -> p (b e u)").bitcast(BF16),
            )

        interleave(False, user_grouped[1][:], user_cols[:])
        for h in range(2):
            quantize_half(h, user_codes, user_scales, user_grouped)
        for c in range(CHUNKS):
            larger(c)
        for c in range(CHUNKS):
            weigh(c)
        turn_values(0, CHUNKS + 2)
        quantize(table_codes[:], table_scales[:], table_grouped[:].rearrange("p j t -> p (j t)"))
        quantize_values(0)
        turn_values(1, CHUNKS + 1)

        sums = []

        def multiply(b):
            acc = bank([P, J], b)
            nc.tensor.matmul_mx(
                out=acc[:],
                lhsT=val_codes[b].bitcast(FP8X4),
                lhsT_scale=val_scales[:, b * P : (b + 1) * P],
                rhs=table_codes[:].bitcast(FP8X4),
                rhs_scale=table_scales[:],
                start=True,
                stop=True,
            )
            sums.append(acc)

        def shift(b, j0, j1):
            j0 = max(j0, 1)
            nc.vector.tensor_tensor(shifted[b][:, j0:j1], sums[b][:, j0 - 1 : j1 - 1], mem_rows[:, j0:j1], ALU.mult)

        results = [sb([P, J], F32, "result%d" % b) for b in range(BLOCKS)]

        def finish(b, j0, j1):
            nc.vector.tensor_tensor(results[b][:, j0:j1], sums[b][:, j0:j1], shifted[b][:, j0:j1], ALU.subtract)
            nc.sync.dma_start(out[b * P : (b + 1) * P, j0:j1], results[b][:, j0:j1])

        multiply(0)
        multiply(1)
        shift(0, 0, J)
        shift(1, 0, J)
        finish(0, 0, J)
        quantize_values(1)
        multiply(2)
        multiply(3)
        finish(1, 0, J)
        shift(2, 0, J)
        shift(3, 0, J)
        finish(2, 0, J)
        finish(3, 0, J)
